import numpy as np
import ml_dtypes


def mxq(x, axis, fmt="e4m3"):
    dtype, down = {"e4m3": (ml_dtypes.float8_e4m3fn, 7), "e5m2": (ml_dtypes.float8_e5m2, 14)}[fmt]
    v = np.moveaxis(np.asarray(x, np.float32).astype(ml_dtypes.bfloat16).astype(np.float64), axis, -1)
    blocks = v.reshape(v.shape[:-1] + (-1, 32))
    amax = np.abs(blocks).max(-1, keepdims=True)
    byte = np.maximum(np.where(amax > 0, np.frexp(amax)[1] - 1 + 127, 0) - down, 1)
    scale = np.exp2(byte - 127.0)
    codes = (blocks / scale).astype(np.float32).astype(dtype).astype(np.float64)
    return np.moveaxis((codes * scale).reshape(v.shape), -1, axis)


WIDE = False


def mx_kscale(k):
    if not WIDE:
        return np.ones(k)
    levels = np.array([10, -10, 5, -5, 0])
    if k % 512:
        return np.exp2(np.random.permutation(np.resize(levels, k // 32))).repeat(32)
    a = np.empty((k // 512, 16))
    for p in range(k // 512):
        a[p, :8] = np.random.permutation(np.resize(levels, 8))
        for g in range(8):
            far = levels[np.abs(levels - a[p, g]) >= 10]
            a[p, g + 8] = far[np.random.randint(len(far))]
    return np.exp2(a.ravel()).repeat(32)


def f64(x):
    return np.asarray(x).astype(np.float64)


def striped(idx):
    return np.tile(np.asarray(idx).reshape(-1, 16).T, (8, 1)).astype(np.uint16)


def unstriped(offs):
    return offs[:16].T.reshape(-1).astype(np.int64)


B, N, T, D, NQ = 1, 512, 2048, 512, 256
DV = 512


def setup_inputs():
    n = np.random.standard_normal
    seg = T // B
    idx = np.concatenate([b * seg + np.random.permutation(seg)[:N] for b in range(B)])
    u = mx_kscale(N)
    ut = np.ones(T)
    ut[idx] = u
    return {
        "vT": (n((DV, T)) / ut).astype(np.float32),
        "wT": (np.random.dirichlet(np.ones(N), NQ).T[None] * u[:, None] * 16).astype(np.float32),
        "lm": (np.random.uniform(0.1, 0.9, (B, NQ, 1))).astype(np.float32),
        "pa": (n((B, NQ, DV))).astype(np.float32),
        "offs": striped(idx),
    }


def reference(vT, wT, lm, pa, offs):
    idx = unstriped(offs)
    pick = lambda x, which: x[:, which].reshape(x.shape[0], B, -1).transpose(1, 0, 2)
    wq = mxq(f64(wT), 1, "e4m3")
    o = wq.transpose(0, 2, 1) @ mxq(pick(f64(vT), idx).transpose(0, 2, 1), 1, "e4m3")
    r_ = f64(lm) * o + (1.0 - f64(lm)) * f64(pa)
    return r_

@@ -1,0 +1,147 @@
+from contextlib import ExitStack
+
+import concourse.mybir as mybir
+from concourse.masks import make_identity
+
+N, T, NQ, DV = 512, 2048, 256, 512
+FLOPS = 2 * NQ * N * DV
+
+F32 = mybir.dt.float32
+BF16 = mybir.dt.bfloat16
+U32 = mybir.dt.uint32
+U16 = mybir.dt.uint16
+U8 = mybir.dt.uint8
+FP8X4 = mybir.dt.float8_e4m3fn_x4
+MULT = mybir.AluOpType.mult
+ADD = mybir.AluOpType.add
+COPY = mybir.ActivationFunctionType.Copy
+
+P = 128
+PACK = 4
+HALVES = NQ // P
+BLOCKS = DV // P
+
+
+def tile_attend_wsum_mix_f_seg_kernel(tc, vT, wT, lm, pa, offs, out):
+    nc = tc.nc
+    pa_rows = pa[0].rearrange("(p h) e -> p h e", h=HALVES)
+    out_rows = out[0].rearrange("(p h) e -> p h e", h=HALVES)
+
+    with ExitStack() as ctx:
+        keep = ctx.enter_context(tc.tile_pool(name="keep", bufs=1))
+        psum = ctx.enter_context(tc.psum_pool(name="psum", bufs=1))
+
+        windows = [keep.tile([P, T], F32, name="window%d" % b) for b in range(BLOCKS)]
+        offsets = keep.tile([P, N // 16], U16, name="offsets")
+        w_raw = keep.tile([P, PACK, NQ], F32, name="w_raw")
+        mix = keep.tile([P, HALVES], F32, name="mix")
+        pa_front = keep.tile([P, HALVES, 2 * P], F32, name="pa_front")
+        pa_back = keep.tile([P, HALVES, 2 * P], F32, name="pa_back")
+
+        nc.sync.dma_start(windows[0][:], vT[0:P, :])
+        nc.sync.dma_start(offsets[:], offs)
+        nc.sync.dma_start(w_raw[:], wT[0].rearrange("(p j) q -> p j q", j=PACK))
+        nc.sync.dma_start(mix[:], lm[0].rearrange("(p h) o -> p (h o)", h=HALVES))
+        for b in range(1, BLOCKS):
+            nc.sync.dma_start(windows[b][:], vT[b * P : (b + 1) * P, :])
+        nc.sync.dma_start(pa_back[:], pa_rows[:, :, 2 * P : 4 * P])
+        nc.sync.dma_start(pa_front[:], pa_rows[:, :, 0 : 2 * P])
+
+        ident = keep.tile([P, P], F32, name="ident")
+        make_identity(nc, ident[:])
+
+        rest = keep.tile([P, HALVES], F32, name="rest")
+        nc.vector.tensor_scalar(rest[:], mix[:], -1.0, 1.0, MULT, ADD)
+
+        w_grouped = keep.tile([P, HALVES, P, PACK], BF16, name="w_grouped", align_bytes=64)
+        w_codes = keep.tile([P, NQ], U32, name="w_codes", align_bytes=64)
+        w_scales = keep.tile([P, NQ], U8, name="w_scales", align_bytes=64)
+
+        def quantize_weights():
+            nc.vector.tensor_copy(w_grouped[:], w_raw[:].rearrange("p j (m h) -> p h m j", h=HALVES))
+            nc.vector.quantize_mx(
+                out=w_codes[:].bitcast(FP8X4),
+                scales=w_scales[:],
+                in_=w_grouped[:].rearrange("p h m j -> p (h m j)"),
+            )
+
+        def gather(b):
+            picked = keep.tile([P, N], BF16, name="picked%d" % b, align_bytes=64)
+            nc.vector.tensor_copy(picked[:], windows[b][:].indirect(offsets[:]))
+            return picked
+
+        def turn(b, picked):
+            words = picked[:].bitcast(F32)
+            turned = psum.tile([P, 2, P], F32, name="turned%d" % (b % 2))
+            for u in range(2):
+                nc.tensor.transpose(turned[:, u, :], words[:, u : N // 2 : 2], ident[:])
+            grouped = keep.tile([P, P * PACK], BF16, name="grouped%d" % b, align_bytes=64)
+            nc.scalar.copy(
+                grouped[:].bitcast(F32).rearrange("p (e u) -> p e u", u=2),
+                turned[:].rearrange("p u e -> p e u"),
+            )
+            return grouped
+
+        def quantize_values(b, grouped):
+            codes = keep.tile([P, P], U32, name="v_codes%d" % b, align_bytes=64)
+            scales = keep.tile([P, P], U8, name="v_scales%d" % b, align_bytes=64)
+            nc.vector.quantize_mx(out=codes[:].bitcast(FP8X4), scales=scales[:], in_=grouped[:])
+            return codes, scales
+
+        def multiply(acc, h, codes, scales):
+            rows = slice(h * P, (h + 1) * P)
+            nc.tensor.matmul_mx(
+                out=acc,
+                lhsT=w_codes[:, rows].bitcast(FP8X4),
+                lhsT_scale=w_scales[:, rows],
+                rhs=codes[:].bitcast(FP8X4),
+                rhs_scale=scales[:],
+                start=True,
+                stop=True,
+            )
+
+        acc_front = [psum.tile([P, 2 * P], F32, name="acc_front%d" % h) for h in range(HALVES)]
+        acc_back = [[psum.tile([P, P], F32, name="acc_back%d_%d" % (i, h)) for h in range(HALVES)] for i in range(2)]
+        scaled_front = keep.tile([P, HALVES, 2 * P], F32, name="scaled_front")
+        scaled_back = keep.tile([P, HALVES, 2 * P], F32, name="scaled_back")
+        res_front = keep.tile([P, HALVES, 2 * P], F32, name="res_front")
+        res_back = [keep.tile([P, HALVES, P], F32, name="res_back%d" % i) for i in range(2)]
+
+        for b in range(2):
+            picked = gather(b)
+            if b == 0:
+                quantize_weights()
+            codes, scales = quantize_values(b, turn(b, picked))
+            for h in range(HALVES):
+                multiply(acc_front[h][:, b * P : (b + 1) * P], h, codes, scales)
+        for h in range(HALVES):
+            nc.scalar.activation(scaled_front[:, h, :], acc_front[h][:], COPY, scale=mix[:, h : h + 1])
+
+        codes, scales = quantize_values(2, turn(2, gather(2)))
+        for h in range(HALVES):
+            multiply(acc_back[0][h][:], h, codes, scales)
+
+        picked = gather(3)
+        for h in range(HALVES):
+            nc.scalar.activation(scaled_back[:, h, :], pa_back[:, h, :], COPY, scale=rest[:, h : h + 1])
+        grouped = turn(3, picked)
+
+        def finish_back(i):
+            for h in range(HALVES):
+                nc.vector.scalar_tensor_tensor(
+                    res_back[i][:, h, :], acc_back[i][h][:], mix[:, h : h + 1],
+                    scaled_back[:, h, i * P : (i + 1) * P], MULT, ADD,
+                )
+            nc.sync.dma_start(out_rows[:, :, (2 + i) * P : (3 + i) * P], res_back[i][:])
+
+        for h in range(HALVES):
+            nc.vector.scalar_tensor_tensor(
+                res_front[:, h, :], pa_front[:, h, :], rest[:, h : h + 1], scaled_front[:, h, :], MULT, ADD
+            )
+        nc.sync.dma_start(out_rows[:, :, 0 : 2 * P], res_front[:])
+        finish_back(0)
+
+        codes, scales = quantize_values(3, grouped)
+        for h in range(HALVES):
+            multiply(acc_back[1][h][:], h, codes, scales)
+        finish_back(1)

@@ -20,6 +20,8 @@ P = 128
 PACK = 4
 HALVES = NQ // P
 BLOCKS = DV // P
+LAST = BLOCKS - 1
+FRONT = LAST * P
 
 
 def tile_attend_wsum_mix_f_seg_kernel(tc, vT, wT, lm, pa, offs, out):
@@ -31,117 +33,105 @@ def tile_attend_wsum_mix_f_seg_kernel(tc, vT, wT, lm, pa, offs, out):
         keep = ctx.enter_context(tc.tile_pool(name="keep", bufs=1))
         psum = ctx.enter_context(tc.psum_pool(name="psum", bufs=1))
 
-        windows = [keep.tile([P, T], F32, name="window%d" % b) for b in range(BLOCKS)]
+        windows = [
+            keep.tile([P, T], F32, name="window%d" % b, tag="window%d" % b, align_bytes=64) for b in range(BLOCKS)
+        ]
         offsets = keep.tile([P, N // 16], U16, name="offsets")
-        w_raw = keep.tile([P, PACK, NQ], F32, name="w_raw")
+        w_raw = keep.tile([P, PACK, NQ], F32, name="w_raw", tag="w_raw", align_bytes=64)
         mix = keep.tile([P, HALVES], F32, name="mix")
-        pa_front = keep.tile([P, HALVES, 2 * P], F32, name="pa_front")
-        pa_back = keep.tile([P, HALVES, 2 * P], F32, name="pa_back")
+        other = [keep.tile([P, DV], F32, name="other%d" % h) for h in range(HALVES)]
 
         nc.sync.dma_start(windows[0][:], vT[0:P, :])
         nc.sync.dma_start(offsets[:], offs)
-        nc.sync.dma_start(w_raw[:], wT[0].rearrange("(p j) q -> p j q", j=PACK))
-        nc.sync.dma_start(mix[:], lm[0].rearrange("(p h) o -> p (h o)", h=HALVES))
         for b in range(1, BLOCKS):
             nc.sync.dma_start(windows[b][:], vT[b * P : (b + 1) * P, :])
-        nc.sync.dma_start(pa_back[:], pa_rows[:, :, 2 * P : 4 * P])
-        nc.sync.dma_start(pa_front[:], pa_rows[:, :, 0 : 2 * P])
+        nc.sync.dma_start(w_raw[:], wT[0].rearrange("(p j) q -> p j q", j=PACK))
+        nc.sync.dma_start(mix[:], lm[0].rearrange("(p h) o -> p (h o)", h=HALVES))
+        for h in range(HALVES):
+            nc.sync.dma_start(other[h][:], pa_rows[:, h, :])
 
         ident = keep.tile([P, P], F32, name="ident")
         make_identity(nc, ident[:])
-
-        rest = keep.tile([P, HALVES], F32, name="rest")
-        nc.vector.tensor_scalar(rest[:], mix[:], -1.0, 1.0, MULT, ADD)
-
-        w_grouped = keep.tile([P, HALVES, P, PACK], BF16, name="w_grouped", align_bytes=64)
-        w_codes = keep.tile([P, NQ], U32, name="w_codes", align_bytes=64)
-        w_scales = keep.tile([P, NQ], U8, name="w_scales", align_bytes=64)
-
-        def quantize_weights():
-            nc.vector.tensor_copy(w_grouped[:], w_raw[:].rearrange("p j (m h) -> p h m j", h=HALVES))
-            nc.vector.quantize_mx(
-                out=w_codes[:].bitcast(FP8X4),
-                scales=w_scales[:],
-                in_=w_grouped[:].rearrange("p h m j -> p (h m j)"),
-            )
 
         def gather(b):
             picked = keep.tile([P, N], BF16, name="picked%d" % b, align_bytes=64)
             nc.vector.tensor_copy(picked[:], windows[b][:].indirect(offsets[:]))
             return picked
 
-        def turn(b, picked):
+        def turn(b, picked, grouped):
             words = picked[:].bitcast(F32)
-            turned = psum.tile([P, 2, P], F32, name="turned%d" % (b % 2))
+            turned = psum.tile([P, 2, P], F32, name="turned%d" % b)
             for u in range(2):
                 nc.tensor.transpose(turned[:, u, :], words[:, u : N // 2 : 2], ident[:])
-            grouped = keep.tile([P, P * PACK], BF16, name="grouped%d" % b, align_bytes=64)
             nc.scalar.copy(
-                grouped[:].bitcast(F32).rearrange("p (e u) -> p e u", u=2),
+                grouped.bitcast(F32).rearrange("p (e u) -> p e u", u=2),
                 turned[:].rearrange("p u e -> p e u"),
             )
-            return grouped
 
-        def quantize_values(b, grouped):
-            codes = keep.tile([P, P], U32, name="v_codes%d" % b, align_bytes=64)
-            scales = keep.tile([P, P], U8, name="v_scales%d" % b, align_bytes=64)
+        def quantize(name, grouped, tag):
+            width = grouped.shape[1] // PACK
+            codes = keep.tile([P, width], U32, name=name + "_codes", tag=tag, align_bytes=64)
+            scales = keep.tile([P, width], U8, name=name + "_scales", align_bytes=64)
             nc.vector.quantize_mx(out=codes[:].bitcast(FP8X4), scales=scales[:], in_=grouped[:])
             return codes, scales
 
-        def multiply(acc, h, codes, scales):
-            rows = slice(h * P, (h + 1) * P)
+        def multiply(acc, weights, values):
             nc.tensor.matmul_mx(
-                out=acc,
-                lhsT=w_codes[:, rows].bitcast(FP8X4),
-                lhsT_scale=w_scales[:, rows],
-                rhs=codes[:].bitcast(FP8X4),
-                rhs_scale=scales[:],
+                out=acc[:],
+                lhsT=weights[0][:].bitcast(FP8X4),
+                lhsT_scale=weights[1][:],
+                rhs=values[0][:].bitcast(FP8X4),
+                rhs_scale=values[1][:],
                 start=True,
                 stop=True,
             )
 
-        acc_front = [psum.tile([P, 2 * P], F32, name="acc_front%d" % h) for h in range(HALVES)]
-        acc_back = [[psum.tile([P, P], F32, name="acc_back%d_%d" % (i, h)) for h in range(HALVES)] for i in range(2)]
-        scaled_front = keep.tile([P, HALVES, 2 * P], F32, name="scaled_front")
-        scaled_back = keep.tile([P, HALVES, 2 * P], F32, name="scaled_back")
-        res_front = keep.tile([P, HALVES, 2 * P], F32, name="res_front")
-        res_back = [keep.tile([P, HALVES, P], F32, name="res_back%d" % i) for i in range(2)]
+        acc = [[psum.tile([P, 2 * P], F32, name="acc%d_%d" % (i, h)) for h in range(HALVES)] for i in range(2)]
+        scaled = [keep.tile([P, DV], F32, name="scaled%d" % h) for h in range(HALVES)]
 
+        first = keep.tile([P, 2 * N], BF16, name="first", align_bytes=64)
         for b in range(2):
-            picked = gather(b)
-            if b == 0:
-                quantize_weights()
-            codes, scales = quantize_values(b, turn(b, picked))
-            for h in range(HALVES):
-                multiply(acc_front[h][:, b * P : (b + 1) * P], h, codes, scales)
-        for h in range(HALVES):
-            nc.scalar.activation(scaled_front[:, h, :], acc_front[h][:], COPY, scale=mix[:, h : h + 1])
+            turn(b, gather(b), first[:, b * N : (b + 1) * N])
+        picked2 = gather(2)
+        q_first = quantize("first", first, "window2")
 
-        codes, scales = quantize_values(2, turn(2, gather(2)))
-        for h in range(HALVES):
-            multiply(acc_back[0][h][:], h, codes, scales)
+        picked3 = gather(LAST)
+        w_view = w_raw[:].rearrange("p j (m h) -> p h m j", h=HALVES)
+        w_grouped = [keep.tile([P, N], BF16, name="w_grouped%d" % h, align_bytes=64) for h in range(HALVES)]
+        nc.vector.tensor_copy(w_grouped[0][:].rearrange("p (m j) -> p m j", j=PACK), w_view[:, 0])
+        nc.scalar.copy(w_grouped[1][:].rearrange("p (m j) -> p m j", j=PACK), w_view[:, 1])
+        rest = keep.tile([P, HALVES], F32, name="rest")
+        nc.gpsimd.tensor_scalar(rest[:], mix[:], -1.0, 1.0, MULT, ADD)
+        weights = [quantize("w%d" % h, w_grouped[h], "w_codes%d" % h) for h in range(HALVES)]
 
-        picked = gather(3)
-        for h in range(HALVES):
-            nc.scalar.activation(scaled_back[:, h, :], pa_back[:, h, :], COPY, scale=rest[:, h : h + 1])
-        grouped = turn(3, picked)
+        def scale_other(h):
+            nc.scalar.activation(scaled[h][:], other[h][:], COPY, scale=rest[:, h : h + 1])
 
-        def finish_back(i):
-            for h in range(HALVES):
-                nc.vector.scalar_tensor_tensor(
-                    res_back[i][:, h, :], acc_back[i][h][:], mix[:, h : h + 1],
-                    scaled_back[:, h, i * P : (i + 1) * P], MULT, ADD,
-                )
-            nc.sync.dma_start(out_rows[:, :, (2 + i) * P : (3 + i) * P], res_back[i][:])
+        third = keep.tile([P, N], BF16, name="third", align_bytes=64)
+        turn(2, picked2, third[:])
+        scale_other(0)
+        fourth = keep.tile([P, N], BF16, name="fourth", tag="w_raw", align_bytes=64)
+        turn(LAST, picked3, fourth[:])
+        scale_other(1)
 
         for h in range(HALVES):
-            nc.vector.scalar_tensor_tensor(
-                res_front[:, h, :], pa_front[:, h, :], rest[:, h : h + 1], scaled_front[:, h, :], MULT, ADD
+            multiply(acc[0][h], weights[h], q_first)
+
+        second_codes = keep.tile([P, 2 * P], U32, name="second_codes", tag="window3", align_bytes=64)
+        second_scales = keep.tile([P, 2 * P], U8, name="second_scales", align_bytes=64)
+        for i, grouped in enumerate((third, fourth)):
+            cols = slice(i * P, (i + 1) * P)
+            nc.vector.quantize_mx(
+                out=second_codes[:, cols].bitcast(FP8X4), scales=second_scales[:, cols], in_=grouped[:]
             )
-        nc.sync.dma_start(out_rows[:, :, 0 : 2 * P], res_front[:])
-        finish_back(0)
-
-        codes, scales = quantize_values(3, grouped)
         for h in range(HALVES):
-            multiply(acc_back[1][h][:], h, codes, scales)
-        finish_back(1)
+            multiply(acc[1][h], weights[h], (second_codes, second_scales))
+
+        for i in range(2):
+            cols = slice(i * 2 * P, (i + 1) * 2 * P)
+            for h in range(HALVES):
+                res = keep.tile([P, 2 * P], F32, name="res%d_%d" % (i, h))
+                nc.vector.scalar_tensor_tensor(
+                    res[:], acc[i][h][:], mix[:, h : h + 1], scaled[h][:, cols], MULT, ADD
+                )
+                nc.sync.dma_start(out_rows[:, h, cols], res[:])

@@ -54,7 +54,7 @@ def tile_attend_wsum_mix_f_seg_kernel(tc, vT, wT, lm, pa, offs, out):
         make_identity(nc, ident[:])
 
         def gather(b):
-            picked = keep.tile([P, N], BF16, name="picked%d" % b, align_bytes=64)
+            picked = keep.tile([P, N], BF16, name="picked%d" % b, tag="picked%d" % b, align_bytes=64)
             nc.vector.tensor_copy(picked[:], windows[b][:].indirect(offsets[:]))
             return picked
 
@@ -87,7 +87,6 @@ def tile_attend_wsum_mix_f_seg_kernel(tc, vT, wT, lm, pa, offs, out):
             )
 
         acc = [[psum.tile([P, 2 * P], F32, name="acc%d_%d" % (i, h)) for h in range(HALVES)] for i in range(2)]
-        scaled = [keep.tile([P, DV], F32, name="scaled%d" % h) for h in range(HALVES)]
 
         first = keep.tile([P, 2 * N], BF16, name="first", align_bytes=64)
         for b in range(2):
@@ -104,15 +103,14 @@ def tile_attend_wsum_mix_f_seg_kernel(tc, vT, wT, lm, pa, offs, out):
         nc.gpsimd.tensor_scalar(rest[:], mix[:], -1.0, 1.0, MULT, ADD)
         weights = [quantize("w%d" % h, w_grouped[h], "w_codes%d" % h) for h in range(HALVES)]
 
-        def scale_other(h):
-            nc.scalar.activation(scaled[h][:], other[h][:], COPY, scale=rest[:, h : h + 1])
-
         third = keep.tile([P, N], BF16, name="third", align_bytes=64)
         turn(2, picked2, third[:])
-        scale_other(0)
+        scaled = [keep.tile([P, DV], F32, name="scaled0")]
+        nc.vector.tensor_scalar(scaled[0][:], other[0][:], rest[:, 0:1], None, MULT)
         fourth = keep.tile([P, N], BF16, name="fourth", tag="w_raw", align_bytes=64)
         turn(LAST, picked3, fourth[:])
-        scale_other(1)
+        scaled.append(keep.tile([P, DV], F32, name="scaled1", tag="picked3", align_bytes=64))
+        nc.scalar.activation(scaled[1][:], other[1][:], COPY, scale=rest[:, 1:2])
 
         for h in range(HALVES):
             multiply(acc[0][h], weights[h], q_first)

from contextlib import ExitStack

import concourse.mybir as mybir
from concourse.masks import make_identity

N, T, NQ, DV = 512, 2048, 256, 512
FLOPS = 2 * NQ * N * DV

F32 = mybir.dt.float32
BF16 = mybir.dt.bfloat16
U32 = mybir.dt.uint32
U16 = mybir.dt.uint16
U8 = mybir.dt.uint8
FP8X4 = mybir.dt.float8_e4m3fn_x4
MULT = mybir.AluOpType.mult
ADD = mybir.AluOpType.add
COPY = mybir.ActivationFunctionType.Copy

P = 128
PACK = 4
HALVES = NQ // P
BLOCKS = DV // P
LAST = BLOCKS - 1
FRONT = LAST * P


def tile_attend_wsum_mix_f_seg_kernel(tc, vT, wT, lm, pa, offs, out):
    nc = tc.nc
    pa_rows = pa[0].rearrange("(p h) e -> p h e", h=HALVES)
    out_rows = out[0].rearrange("(p h) e -> p h e", h=HALVES)

    with ExitStack() as ctx:
        keep = ctx.enter_context(tc.tile_pool(name="keep", bufs=1))
        psum = ctx.enter_context(tc.psum_pool(name="psum", bufs=1))

        windows = [
            keep.tile([P, T], F32, name="window%d" % b, tag="window%d" % b, align_bytes=64) for b in range(BLOCKS)
        ]
        offsets = keep.tile([P, N // 16], U16, name="offsets")
        w_raw = keep.tile([P, PACK, NQ], F32, name="w_raw", tag="w_raw", align_bytes=64)
        mix = keep.tile([P, HALVES], F32, name="mix")
        other = [keep.tile([P, DV], F32, name="other%d" % h) for h in range(HALVES)]

        nc.sync.dma_start(windows[0][:], vT[0:P, :])
        nc.sync.dma_start(offsets[:], offs)
        for b in range(1, BLOCKS):
            nc.sync.dma_start(windows[b][:], vT[b * P : (b + 1) * P, :])
        nc.sync.dma_start(w_raw[:], wT[0].rearrange("(p j) q -> p j q", j=PACK))
        nc.sync.dma_start(mix[:], lm[0].rearrange("(p h) o -> p (h o)", h=HALVES))
        for h in range(HALVES):
            nc.sync.dma_start(other[h][:], pa_rows[:, h, :])

        ident = keep.tile([P, P], F32, name="ident")
        make_identity(nc, ident[:])

        def gather(b):
            picked = keep.tile([P, N], BF16, name="picked%d" % b, tag="picked%d" % b, align_bytes=64)
            nc.vector.tensor_copy(picked[:], windows[b][:].indirect(offsets[:]))
            return picked

        def turn(b, picked, grouped):
            words = picked[:].bitcast(F32)
            turned = psum.tile([P, 2, P], F32, name="turned%d" % b)
            for u in range(2):
                nc.tensor.transpose(turned[:, u, :], words[:, u : N // 2 : 2], ident[:])
            nc.scalar.copy(
                grouped.bitcast(F32).rearrange("p (e u) -> p e u", u=2),
                turned[:].rearrange("p u e -> p e u"),
            )

        def quantize(name, grouped, tag):
            width = grouped.shape[1] // PACK
            codes = keep.tile([P, width], U32, name=name + "_codes", tag=tag, align_bytes=64)
            scales = keep.tile([P, width], U8, name=name + "_scales", align_bytes=64)
            nc.vector.quantize_mx(out=codes[:].bitcast(FP8X4), scales=scales[:], in_=grouped[:])
            return codes, scales

        def multiply(acc, weights, values):
            nc.tensor.matmul_mx(
                out=acc[:],
                lhsT=weights[0][:].bitcast(FP8X4),
                lhsT_scale=weights[1][:],
                rhs=values[0][:].bitcast(FP8X4),
                rhs_scale=values[1][:],
                start=True,
                stop=True,
            )

        acc = [[psum.tile([P, 2 * P], F32, name="acc%d_%d" % (i, h)) for h in range(HALVES)] for i in range(2)]

        first = keep.tile([P, 2 * N], BF16, name="first", align_bytes=64)
        for b in range(2):
            turn(b, gather(b), first[:, b * N : (b + 1) * N])
        picked2 = gather(2)
        q_first = quantize("first", first, "window2")

        picked3 = gather(LAST)
        w_view = w_raw[:].rearrange("p j (m h) -> p h m j", h=HALVES)
        w_grouped = [keep.tile([P, N], BF16, name="w_grouped%d" % h, align_bytes=64) for h in range(HALVES)]
        nc.vector.tensor_copy(w_grouped[0][:].rearrange("p (m j) -> p m j", j=PACK), w_view[:, 0])
        nc.scalar.copy(w_grouped[1][:].rearrange("p (m j) -> p m j", j=PACK), w_view[:, 1])
        rest = keep.tile([P, HALVES], F32, name="rest")
        nc.gpsimd.tensor_scalar(rest[:], mix[:], -1.0, 1.0, MULT, ADD)
        weights = [quantize("w%d" % h, w_grouped[h], "w_codes%d" % h) for h in range(HALVES)]

        third = keep.tile([P, N], BF16, name="third", align_bytes=64)
        turn(2, picked2, third[:])
        scaled = [keep.tile([P, DV], F32, name="scaled0")]
        nc.vector.tensor_scalar(scaled[0][:], other[0][:], rest[:, 0:1], None, MULT)
        fourth = keep.tile([P, N], BF16, name="fourth", tag="w_raw", align_bytes=64)
        turn(LAST, picked3, fourth[:])
        scaled.append(keep.tile([P, DV], F32, name="scaled1", tag="picked3", align_bytes=64))
        nc.scalar.activation(scaled[1][:], other[1][:], COPY, scale=rest[:, 1:2])

        for h in range(HALVES):
            multiply(acc[0][h], weights[h], q_first)

        second_codes = keep.tile([P, 2 * P], U32, name="second_codes", tag="window3", align_bytes=64)
        second_scales = keep.tile([P, 2 * P], U8, name="second_scales", align_bytes=64)
        for i, grouped in enumerate((third, fourth)):
            cols = slice(i * P, (i + 1) * P)
            nc.vector.quantize_mx(
                out=second_codes[:, cols].bitcast(FP8X4), scales=second_scales[:, cols], in_=grouped[:]
            )
        for h in range(HALVES):
            multiply(acc[1][h], weights[h], (second_codes, second_scales))

        for i in range(2):
            cols = slice(i * 2 * P, (i + 1) * 2 * P)
            for h in range(HALVES):
                res = keep.tile([P, 2 * P], F32, name="res%d_%d" % (i, h))
                nc.vector.scalar_tensor_tensor(
                    res[:], acc[i][h][:], mix[:, h : h + 1], scaled[h][:, cols], MULT, ADD
                )
                nc.sync.dma_start(out_rows[:, h, cols], res[:])
